import numpy as np, ml_dtypes
CORES = [0,1,2,3]
N = 4
def setup_inputs(rng):
    return {"x1": rng.standard_normal((N, 128, 32), dtype=np.float32), "x2": rng.standard_normal((N, 128, 2048), dtype=np.float32).astype(ml_dtypes.bfloat16)}
def reference(x1, x2):
    out = []
    g = np.concatenate(list(x1), axis=1)
    out.append(np.broadcast_to(g, (N,) + g.shape))
    s = x2.sum(axis=0, dtype=np.float64).astype(x2.dtype)
    b = 2048 // N
    out.append(np.stack([s[:, r * b:(r + 1) * b] for r in range(N)]))
    return {"y1": out[0], "y2": out[1]}

from concourse.bass import DstId, RemoteDMATransfer
from concourse.mybir import AluOpType

N = 4
W1 = 32
B = 512

SCRATCH = {
    "gat": ("sbuf", [128, N * W1], "float32"),
    "xs": ("sbuf", [128, N * B], "bfloat16"),
    "land": ("sbuf", [128, N * B], "bfloat16"),
}
SEMAPHORES = [
    "ld1",
    "ld2",
    "own",
    "sent",
    "arr1",
    "arr2",
    "add",
    "st1",
]

ALL = 0xFFFF


def rank_program(g, core, T, topo):
    r = T.rank_of(core)
    if r is None:
        return
    S = T.sem
    others = [j for j in range(N) if j != r]

    def blk(t, j):
        return t[:, j * B:(j + 1) * B]

    mine1 = T.gat[:, r * W1:(r + 1) * W1]

    g.scalar.dma_start(mine1, T.x1[:]).then_inc(S.ld1, 16)
    g.sync.dma_start(T.xs[:], T.x2[:]).then_inc(S.ld2, 16)
    g.sync.dma_start(T.y2[:], blk(T.x2, r)).then_inc(S.own, 16)

    g.wait_ge(S.ld1, 16)
    ids = []
    for j in others:
        rid, pid, _se = topo.addr(T.cores[j])
        ids.append(DstId(rid=rid, pnc=pid))
    g.remote_dma_fused(
        [RemoteDMATransfer(dst_ids=ids, dma_engine_mask=ALL, remote_sem=S.arr1,
                           srcs=[mine1], dsts=[mine1 for _ in others])],
        local_sem=S.sent)

    g.wait_ge(S.ld2, 16)
    for k in range(1, N):
        j = (r + k) % N
        rid, pid, _se = topo.addr(T.cores[j])
        g.remote_dma(blk(T.land, r), blk(T.xs, j), S.arr2, S.sent, pid, rid, ALL)

    g.scalar.wait_ge(S.ld1, 16)
    g.scalar.wait_ge(S.arr1, 16 * (N - 1))
    g.scalar.dma_start(T.y1[:], T.gat[:]).then_inc(S.st1, 16)

    a, b, c = others
    g.wait_ge(S.arr2, 16 * (N - 1))
    g.wait_ge(S.own, 16)
    g.dma_start(blk(T.land, a), blk(T.land, b), accum_op=AluOpType.add).then_inc(S.add, 16)
    g.dma_start(T.y2[:], blk(T.land, c), accum_op=AluOpType.add).then_inc(S.add, 16)
    g.wait_ge(S.add, 32)
    g.dma_start(T.y2[:], blk(T.land, a), accum_op=AluOpType.add).then_inc(S.add, 16)
    g.wait_ge(S.add, 48)

    g.wait_ge(S.sent, 16 * N)
    g.wait_ge(S.arr1, 16 * (N - 1))
    g.wait_ge(S.st1, 16)
